import numpy as np
import ml_dtypes


def mxq(x, axis, fmt="e4m3"):
    dtype, down = {"e4m3": (ml_dtypes.float8_e4m3fn, 7), "e5m2": (ml_dtypes.float8_e5m2, 14)}[fmt]
    v = np.moveaxis(np.asarray(x, np.float32).astype(ml_dtypes.bfloat16).astype(np.float64), axis, -1)
    blocks = v.reshape(v.shape[:-1] + (-1, 32))
    amax = np.abs(blocks).max(-1, keepdims=True)
    byte = np.maximum(np.where(amax > 0, np.frexp(amax)[1] - 1 + 127, 0) - down, 1)
    scale = np.exp2(byte - 127.0)
    codes = (blocks / scale).astype(np.float32).astype(dtype).astype(np.float64)
    return np.moveaxis((codes * scale).reshape(v.shape), -1, axis)


WIDE = False


def mx_kscale(k, group=512):
    if not WIDE:
        return np.ones(k)
    levels = np.array([18, -18])
    if group != 512:
        return np.exp2(np.random.permutation(np.resize(levels, k // group))).repeat(group)
    if k % 512:
        return np.exp2(np.random.permutation(np.resize(levels, k // 32))).repeat(32)
    a = np.empty((k // 512, 16))
    for p in range(k // 512):
        a[p, :8] = np.random.permutation(np.resize(levels, 8))
        for g in range(8):
            far = levels[np.abs(levels - a[p, g]) >= 10]
            a[p, g + 8] = far[np.random.randint(len(far))]
    return np.exp2(a.ravel()).repeat(32)


def f64(x):
    return np.asarray(x).astype(np.float64)


E2M1 = np.array([0.0, 0.5, 1.0, 1.5, 2.0, 3.0, 4.0, 6.0, -0.0, -0.5, -1.0, -1.5, -2.0, -3.0, -4.0, -6.0])


def pack_group(w):
    k, n = w.shape
    w = f64(np.asarray(w, np.float32).astype(ml_dtypes.bfloat16)).reshape(k // 32, 32, n)
    amax = np.abs(w).max(1)
    mant, ex = np.frexp(amax / 6.0)
    byte = np.clip(np.where(amax > 0, np.where(mant > 0.5, ex, ex - 1) + 127, 1), 1, 254)
    scaled = (w * np.exp2(127.0 - byte)[:, None, :]).reshape(k, n).astype(np.float32)
    c = np.ascontiguousarray(scaled.reshape(k // 4, 4, n).transpose(0, 2, 1)).astype(ml_dtypes.float4_e2m1fn).view(np.uint8) & 0xF
    return np.ascontiguousarray((c[..., 0::2] | (c[..., 1::2] << 4)).reshape(k // 4, 2 * n)), byte.astype(np.uint8)


def unpack_group(words, scales):
    p, n = words.shape[0], scales.shape[1]
    words = np.ascontiguousarray(words).reshape(p, n, 2)
    nib = np.empty((p, n, 4), np.uint8)
    nib[..., 0::2] = words & 0xF
    nib[..., 1::2] = words >> 4
    return E2M1[nib].transpose(0, 2, 1).reshape(4 * p, n) * np.repeat(np.exp2(scales.astype(np.float64) - 127.0), 32, axis=0)


G, D, M, N = 8, 128, 128, 512


def setup_inputs():
    n = np.random.standard_normal
    s = mx_kscale(D, 0)[:, None]
    w_ = [pack_group(w) for w in n((G, D, M)) / np.sqrt(D) / s]
    return {
        "x": (n((G, D, N)) * s).astype(np.float32),
        "w_words": np.stack([w[0] for w in w_]),
        "w_scales": np.stack([w[1] for w in w_]),
    }


def reference(x, w_words, w_scales):
    xq = mxq(f64(x), 1, "e4m3")
    y = np.stack([unpack_group(w_words[g], w_scales[g]) for g in range(G)]).transpose(0, 2, 1) @ xq
    return y

@@ -1,0 +1,119 @@
+from contextlib import ExitStack
+
+import concourse.mybir as mybir
+
+G, D, M, N = 8, 128, 128, 512
+FLOPS = 2 * G * D * M * N
+
+F32 = mybir.dt.float32
+BF16 = mybir.dt.bfloat16
+I32 = mybir.dt.int32
+U8 = mybir.dt.uint8
+FP8X4 = mybir.dt.float8_e4m3fn_x4
+FP4X4 = mybir.dt.float4_e2m1fn_x4
+
+P = 128
+PACK = 4
+ROWS = 32
+SIDE = 4
+SETS = 2
+UNITS = [[0,0,256],[0,256,256],[1,0,256],[1,256,256]]
+ILV = [192,192,192,192]
+SEQ = [["i",0,"V"],["i",0,"S"],["q",0],["m",0],["i",1,"V"],["i",1,"S"],["q",1],["m",1],["e",0,0,"S"],["e",0,1,"S"],["s",0,0,2],["e",0,3,"S"],["i",2,"V"],["i",2,"S"],["e",0,2,"V"],["s",0,2,4],["q",2],["m",2],["e",1,2,"V"],["e",1,3,"S"],["s",1,2,4],["i",3,"V"],["i",3,"S"],["e",1,1,"V"],["e",1,0,"S"],["s",1,0,2],["q",3],["m",3],["e",2,1,"V"],["e",2,0,"S"],["e",2,2,"V"],["e",2,3,"S"],["s",2,0,4],["e",3,1,"V"],["e",3,0,"S"],["s",3,0,2],["e",3,2,"V"],["e",3,3,"S"],["s",3,2,4]]
+NSM = 1
+PAD = N - UNITS[0][2]
+
+
+def tile_rows_glin_kernel(tc, x, w_words, w_scales, out):
+    nc = tc.nc
+    with ExitStack() as ctx:
+        sb = ctx.enter_context(tc.tile_pool(name="sb", bufs=1))
+        ps = ctx.enter_context(tc.psum_pool(name="ps", bufs=1))
+        ctx.enter_context(tc.manual_schedule())
+
+        words = sb.tile([P, SETS, 2 * M], U8, name="words", align_bytes=64)
+        wsc = sb.tile([P, SETS, M], U8, name="wsc", align_bytes=64)
+        codes = sb.tile([P, PAD + SETS * N], I32, name="codes", align_bytes=64)
+        xsc = sb.tile([P, PAD + SETS * N], U8, name="xsc", align_bytes=64)
+        raw = [sb.tile([P, PACK, w], F32, name="raw%d" % u, align_bytes=64) for u, (s, c0, w) in enumerate(UNITS)]
+        grp = [sb.tile([P, w, PACK], BF16, name="grp%d" % u, align_bytes=64) for u, (s, c0, w) in enumerate(UNITS)]
+        res = [sb.tile([P, SIDE, w], F32, name="res%d" % u, align_bytes=64) for u, (s, c0, w) in enumerate(UNITS)]
+        banks = [[ps.tile([P, N], F32, name="bank%d_%d" % (c, h)) for h in range(2)] for c in range(SIDE)]
+
+        nc.vector.memset(wsc[:].bitcast(I32), 0)
+        if PAD:
+            nc.vector.memset(codes[:, 0:PAD], 0)
+            nc.vector.memset(xsc[:, 0:PAD].bitcast(I32), 0)
+
+        x_rows = x.rearrange("g d n -> (g d) n")
+        for u, (s, c0, w) in enumerate(UNITS):
+            src = x_rows[s * P * PACK : (s + 1) * P * PACK, :].rearrange("(q j) n -> q j n", j=PACK)
+            nc.sync.dma_start(out=raw[u][:], in_=src[:, :, c0 : c0 + w])
+            if u == NSM - 1:
+                nc.sync.dma_start(
+                    out=words[:].bitcast(I32),
+                    in_=w_words.rearrange("g p b -> (g p) b").rearrange("(s q) b -> q s b", s=SETS).bitcast(I32),
+                )
+                for f in range(4):
+                    nc.sync.dma_start(
+                        out=wsc[:].bitcast(I32)[f:P:ROWS],
+                        in_=w_scales.rearrange("(s c) f m -> f c s m", s=SETS)[f].bitcast(I32),
+                    )
+
+        def interleave(u, eng):
+            w = UNITS[u][2]
+            a, b = (0, ILV[u]) if eng == "V" else (ILV[u], w)
+            dst = grp[u][:, a:b, :].rearrange("p (c i) t -> p c t i", i=4)
+            src = raw[u][:, :, a:b].rearrange("p t (c i) -> p c t i", i=4)
+            if eng == "V":
+                nc.vector.tensor_copy(out=dst, in_=src)
+            else:
+                nc.scalar.copy(out=dst, in_=src)
+
+        def quantize(u):
+            s, c0, w = UNITS[u]
+            at = PAD + s * N + c0
+            nc.vector.quantize_mx(
+                out=codes[:, at : at + w].bitcast(FP8X4),
+                scales=xsc[:, at : at + w],
+                in_=grp[u][:].rearrange("p n t -> p (n t)"),
+            )
+
+        def multiply(u):
+            s, c0, w = UNITS[u]
+            end = PAD + s * N + c0 + w
+            for c in range(SIDE):
+                rows = slice(ROWS * c, ROWS * (c + 1))
+                nc.tensor.matmul_mx(
+                    out=banks[c][u % 2][:],
+                    lhsT=words[rows, s, :].bitcast(FP4X4),
+                    lhsT_scale=wsc[rows, s, :],
+                    rhs=codes[rows, end - N : end].bitcast(FP8X4),
+                    rhs_scale=xsc[rows, end - N : end],
+                    start=True,
+                    stop=True,
+                )
+
+        def empty(u, c, eng):
+            w = UNITS[u][2]
+            if eng == "V":
+                nc.vector.tensor_copy(out=res[u][:, c, :], in_=banks[c][u % 2][:, N - w : N])
+            else:
+                nc.scalar.copy(out=res[u][:, c, :], in_=banks[c][u % 2][:, N - w : N])
+
+        def store(u, ca, cb):
+            s, c0, w = UNITS[u]
+            dst = out[SIDE * s + ca : SIDE * s + cb, :, c0 : c0 + w].rearrange("c m n -> m c n")
+            nc.sync.dma_start(out=dst, in_=res[u][:, ca:cb, :])
+
+        for step in SEQ:
+            if step[0] == "i":
+                interleave(step[1], step[2])
+            elif step[0] == "q":
+                quantize(step[1])
+            elif step[0] == "m":
+                multiply(step[1])
+            elif step[0] == "e":
+                empty(step[1], step[2], step[3])
+            else:
+                store(step[1], step[2], step[3])

@@ -17,11 +17,10 @@ PACK = 4
 ROWS = 32
 SIDE = 4
 SETS = 2
-UNITS = [[0,0,256],[0,256,256],[1,0,256],[1,256,256]]
-ILV = [192,192,192,192]
-SEQ = [["i",0,"V"],["i",0,"S"],["q",0],["m",0],["i",1,"V"],["i",1,"S"],["q",1],["m",1],["e",0,0,"S"],["e",0,1,"S"],["s",0,0,2],["e",0,3,"S"],["i",2,"V"],["i",2,"S"],["e",0,2,"V"],["s",0,2,4],["q",2],["m",2],["e",1,2,"V"],["e",1,3,"S"],["s",1,2,4],["i",3,"V"],["i",3,"S"],["e",1,1,"V"],["e",1,0,"S"],["s",1,0,2],["q",3],["m",3],["e",2,1,"V"],["e",2,0,"S"],["e",2,2,"V"],["e",2,3,"S"],["s",2,0,4],["e",3,1,"V"],["e",3,0,"S"],["s",3,0,2],["e",3,2,"V"],["e",3,3,"S"],["s",3,2,4]]
-NSM = 1
-PAD = N - UNITS[0][2]
+W = 256
+PIECES = SETS * N // W
+SPLIT = 176
+PAD = N - W
 
 
 def tile_rows_glin_kernel(tc, x, w_words, w_scales, out):
@@ -35,53 +34,52 @@ def tile_rows_glin_kernel(tc, x, w_words, w_scales, out):
         wsc = sb.tile([P, SETS, M], U8, name="wsc", align_bytes=64)
         codes = sb.tile([P, PAD + SETS * N], I32, name="codes", align_bytes=64)
         xsc = sb.tile([P, PAD + SETS * N], U8, name="xsc", align_bytes=64)
-        raw = [sb.tile([P, PACK, w], F32, name="raw%d" % u, align_bytes=64) for u, (s, c0, w) in enumerate(UNITS)]
-        grp = [sb.tile([P, w, PACK], BF16, name="grp%d" % u, align_bytes=64) for u, (s, c0, w) in enumerate(UNITS)]
-        res = [sb.tile([P, SIDE, w], F32, name="res%d" % u, align_bytes=64) for u, (s, c0, w) in enumerate(UNITS)]
+        raw = [sb.tile([P, PACK, W], F32, name="raw%d" % u, align_bytes=64) for u in range(PIECES)]
+        grp = [sb.tile([P, W, PACK], BF16, name="grp%d" % u, align_bytes=64) for u in range(PIECES)]
+        res = [sb.tile([P, SIDE, W], F32, name="res%d" % u, align_bytes=64) for u in range(PIECES)]
         banks = [[ps.tile([P, N], F32, name="bank%d_%d" % (c, h)) for h in range(2)] for c in range(SIDE)]
 
-        nc.vector.memset(wsc[:].bitcast(I32), 0)
-        if PAD:
-            nc.vector.memset(codes[:, 0:PAD], 0)
-            nc.vector.memset(xsc[:, 0:PAD].bitcast(I32), 0)
+        nc.vector.memset(codes[:, 0:PAD], 0)
+        nc.vector.memset(xsc[:, 0:PAD].bitcast(I32), 0)
 
         x_rows = x.rearrange("g d n -> (g d) n")
-        for u, (s, c0, w) in enumerate(UNITS):
-            src = x_rows[s * P * PACK : (s + 1) * P * PACK, :].rearrange("(q j) n -> q j n", j=PACK)
-            nc.sync.dma_start(out=raw[u][:], in_=src[:, :, c0 : c0 + w])
-            if u == NSM - 1:
-                nc.sync.dma_start(
-                    out=words[:].bitcast(I32),
-                    in_=w_words.rearrange("g p b -> (g p) b").rearrange("(s q) b -> q s b", s=SETS).bitcast(I32),
-                )
-                for f in range(4):
-                    nc.sync.dma_start(
-                        out=wsc[:].bitcast(I32)[f:P:ROWS],
-                        in_=w_scales.rearrange("(s c) f m -> f c s m", s=SETS)[f].bitcast(I32),
-                    )
 
-        def interleave(u, eng):
-            w = UNITS[u][2]
-            a, b = (0, ILV[u]) if eng == "V" else (ILV[u], w)
-            dst = grp[u][:, a:b, :].rearrange("p (c i) t -> p c t i", i=4)
-            src = raw[u][:, :, a:b].rearrange("p t (c i) -> p c t i", i=4)
-            if eng == "V":
-                nc.vector.tensor_copy(out=dst, in_=src)
-            else:
-                nc.scalar.copy(out=dst, in_=src)
+        def load(u):
+            s, c0 = divmod(u * W, N)
+            src = x_rows[s * P * PACK : (s + 1) * P * PACK, :].rearrange("(q j) n -> q j n", j=PACK)
+            nc.sync.dma_start(out=raw[u][:], in_=src[:, :, c0 : c0 + W])
+
+        load(0)
+        nc.sync.dma_start(
+            out=words[:].bitcast(I32),
+            in_=w_words.rearrange("g p b -> (g p) b").rearrange("(s q) b -> q s b", s=SETS).bitcast(I32),
+        )
+        for f in range(4):
+            nc.sync.dma_start(
+                out=wsc[:].bitcast(I32)[f:P:ROWS],
+                in_=w_scales.rearrange("(s c) f m -> f c s m", s=SETS)[f].bitcast(I32),
+            )
+        for u in range(1, PIECES):
+            load(u)
+
+        def interleave(u):
+            for a, b, copy in ((0, SPLIT, nc.vector.tensor_copy), (SPLIT, W, nc.scalar.copy)):
+                copy(
+                    out=grp[u][:, a:b, :].rearrange("p (c i) t -> p c t i", i=4),
+                    in_=raw[u][:, :, a:b].rearrange("p t (c i) -> p c t i", i=4),
+                )
 
         def quantize(u):
-            s, c0, w = UNITS[u]
-            at = PAD + s * N + c0
+            at = PAD + u * W
             nc.vector.quantize_mx(
-                out=codes[:, at : at + w].bitcast(FP8X4),
-                scales=xsc[:, at : at + w],
+                out=codes[:, at : at + W].bitcast(FP8X4),
+                scales=xsc[:, at : at + W],
                 in_=grp[u][:].rearrange("p n t -> p (n t)"),
             )
 
         def multiply(u):
-            s, c0, w = UNITS[u]
-            end = PAD + s * N + c0 + w
+            s = u * W // N
+            end = PAD + (u + 1) * W
             for c in range(SIDE):
                 rows = slice(ROWS * c, ROWS * (c + 1))
                 nc.tensor.matmul_mx(
@@ -94,26 +92,19 @@ def tile_rows_glin_kernel(tc, x, w_words, w_scales, out):
                     stop=True,
                 )
 
-        def empty(u, c, eng):
-            w = UNITS[u][2]
-            if eng == "V":
-                nc.vector.tensor_copy(out=res[u][:, c, :], in_=banks[c][u % 2][:, N - w : N])
-            else:
-                nc.scalar.copy(out=res[u][:, c, :], in_=banks[c][u % 2][:, N - w : N])
+        def empty(u, on_vector):
+            s, c0 = divmod(u * W, N)
+            for c in range(SIDE):
+                copy = nc.vector.tensor_copy if c in on_vector else nc.scalar.copy
+                copy(out=res[u][:, c, :], in_=banks[c][u % 2][:, N - W : N])
+                if c % 2 == 1:
+                    dst = out[SIDE * s + c - 1 : SIDE * s + c + 1, :, c0 : c0 + W].rearrange("c m n -> m c n")
+                    nc.sync.dma_start(out=dst, in_=res[u][:, c - 1 : c + 1, :])
 
-        def store(u, ca, cb):
-            s, c0, w = UNITS[u]
-            dst = out[SIDE * s + ca : SIDE * s + cb, :, c0 : c0 + w].rearrange("c m n -> m c n")
-            nc.sync.dma_start(out=dst, in_=res[u][:, ca:cb, :])
-
-        for step in SEQ:
-            if step[0] == "i":
-                interleave(step[1], step[2])
-            elif step[0] == "q":
-                quantize(step[1])
-            elif step[0] == "m":
-                multiply(step[1])
-            elif step[0] == "e":
-                empty(step[1], step[2], step[3])
-            else:
-                store(step[1], step[2], step[3])
+        for u in range(PIECES):
+            interleave(u)
+            quantize(u)
+            multiply(u)
+            if u > 0:
+                empty(u - 1, (3,))
+        empty(PIECES - 1, (0, 2))

@@ -19,7 +19,8 @@ SIDE = 4
 SETS = 2
 W = 256
 PIECES = SETS * N // W
-SPLIT = 176
+H = W // 2
+SPLIT = 192
 PAD = N - W
 
 
@@ -63,19 +64,25 @@ def tile_rows_glin_kernel(tc, x, w_words, w_scales, out):
             load(u)
 
         def interleave(u):
-            for a, b, copy in ((0, SPLIT, nc.vector.tensor_copy), (SPLIT, W, nc.scalar.copy)):
+            shares = [(0, H, nc.vector.tensor_copy)]
+            if u < PIECES - 1:
+                shares = shares + [(H, SPLIT, nc.vector.tensor_copy), (SPLIT, W, nc.scalar.copy)]
+            else:
+                shares = shares + [(H, W, nc.vector.tensor_copy)]
+            for a, b, copy in shares:
                 copy(
                     out=grp[u][:, a:b, :].rearrange("p (c i) t -> p c t i", i=4),
                     in_=raw[u][:, :, a:b].rearrange("p t (c i) -> p c t i", i=4),
                 )
 
         def quantize(u):
-            at = PAD + u * W
-            nc.vector.quantize_mx(
-                out=codes[:, at : at + W].bitcast(FP8X4),
-                scales=xsc[:, at : at + W],
-                in_=grp[u][:].rearrange("p n t -> p (n t)"),
-            )
+            for a in (0, H):
+                at = PAD + u * W + a
+                nc.vector.quantize_mx(
+                    out=codes[:, at : at + H].bitcast(FP8X4),
+                    scales=xsc[:, at : at + H],
+                    in_=grp[u][:, a : a + H, :].rearrange("p n t -> p (n t)"),
+                )
 
         def multiply(u):
             s = u * W // N
@@ -106,5 +113,5 @@ def tile_rows_glin_kernel(tc, x, w_words, w_scales, out):
             quantize(u)
             multiply(u)
             if u > 0:
-                empty(u - 1, (3,))
-        empty(PIECES - 1, (0, 2))
+                empty(u - 1, (1,))
+        empty(PIECES - 1, (1, 3))

@@ -17,11 +17,11 @@ PACK = 4
 ROWS = 32
 SIDE = 4
 SETS = 2
-W = 256
-PIECES = SETS * N // W
-H = W // 2
-SPLIT = 192
-PAD = N - W
+CALLS = [(128, 128)] * 4
+WIDTH = [sum(calls) for calls in CALLS]
+START = [sum(WIDTH[:u]) for u in range(len(WIDTH))]
+PIECES = len(WIDTH)
+PAD = N - WIDTH[0]
 
 
 def tile_rows_glin_kernel(tc, x, w_words, w_scales, out):
@@ -35,9 +35,9 @@ def tile_rows_glin_kernel(tc, x, w_words, w_scales, out):
         wsc = sb.tile([P, SETS, M], U8, name="wsc", align_bytes=64)
         codes = sb.tile([P, PAD + SETS * N], I32, name="codes", align_bytes=64)
         xsc = sb.tile([P, PAD + SETS * N], U8, name="xsc", align_bytes=64)
-        raw = [sb.tile([P, PACK, W], F32, name="raw%d" % u, align_bytes=64) for u in range(PIECES)]
-        grp = [sb.tile([P, W, PACK], BF16, name="grp%d" % u, align_bytes=64) for u in range(PIECES)]
-        res = [sb.tile([P, SIDE, W], F32, name="res%d" % u, align_bytes=64) for u in range(PIECES)]
+        raw = [sb.tile([P, PACK, w], F32, name="raw%d" % u, align_bytes=64) for u, w in enumerate(WIDTH)]
+        grp = [sb.tile([P, w, PACK], BF16, name="grp%d" % u, align_bytes=64) for u, w in enumerate(WIDTH)]
+        res = [sb.tile([P, SIDE, w], F32, name="res%d" % u, align_bytes=64) for u, w in enumerate(WIDTH)]
         banks = [[ps.tile([P, N], F32, name="bank%d_%d" % (c, h)) for h in range(2)] for c in range(SIDE)]
 
         nc.vector.memset(codes[:, 0:PAD], 0)
@@ -46,9 +46,9 @@ def tile_rows_glin_kernel(tc, x, w_words, w_scales, out):
         x_rows = x.rearrange("g d n -> (g d) n")
 
         def load(u):
-            s, c0 = divmod(u * W, N)
+            s, c0 = divmod(START[u], N)
             src = x_rows[s * P * PACK : (s + 1) * P * PACK, :].rearrange("(q j) n -> q j n", j=PACK)
-            nc.sync.dma_start(out=raw[u][:], in_=src[:, :, c0 : c0 + W])
+            nc.sync.dma_start(out=raw[u][:], in_=src[:, :, c0 : c0 + WIDTH[u]])
 
         load(0)
         nc.sync.dma_start(
@@ -63,30 +63,30 @@ def tile_rows_glin_kernel(tc, x, w_words, w_scales, out):
         for u in range(1, PIECES):
             load(u)
 
-        def interleave(u):
-            shares = [(0, H, nc.vector.tensor_copy)]
-            if u < PIECES - 1:
-                shares = shares + [(H, SPLIT, nc.vector.tensor_copy), (SPLIT, W, nc.scalar.copy)]
-            else:
-                shares = shares + [(H, W, nc.vector.tensor_copy)]
+        def interleave(u, scalar_share):
+            first, split = CALLS[u][0], WIDTH[u] - scalar_share
+            shares = [(0, first, nc.vector.tensor_copy), (first, split, nc.vector.tensor_copy), (split, WIDTH[u], nc.scalar.copy)]
             for a, b, copy in shares:
-                copy(
-                    out=grp[u][:, a:b, :].rearrange("p (c i) t -> p c t i", i=4),
-                    in_=raw[u][:, :, a:b].rearrange("p t (c i) -> p c t i", i=4),
-                )
+                if b > a:
+                    copy(
+                        out=grp[u][:, a:b, :].rearrange("p (c i) t -> p c t i", i=4),
+                        in_=raw[u][:, :, a:b].rearrange("p t (c i) -> p c t i", i=4),
+                    )
 
         def quantize(u):
-            for a in (0, H):
-                at = PAD + u * W + a
+            a = 0
+            for w in CALLS[u]:
+                at = PAD + START[u] + a
                 nc.vector.quantize_mx(
-                    out=codes[:, at : at + H].bitcast(FP8X4),
-                    scales=xsc[:, at : at + H],
-                    in_=grp[u][:, a : a + H, :].rearrange("p n t -> p (n t)"),
+                    out=codes[:, at : at + w].bitcast(FP8X4),
+                    scales=xsc[:, at : at + w],
+                    in_=grp[u][:, a : a + w, :].rearrange("p n t -> p (n t)"),
                 )
+                a = a + w
 
         def multiply(u):
-            s = u * W // N
-            end = PAD + (u + 1) * W
+            s = START[u] // N
+            end = PAD + START[u] + WIDTH[u]
             for c in range(SIDE):
                 rows = slice(ROWS * c, ROWS * (c + 1))
                 nc.tensor.matmul_mx(
@@ -99,19 +99,21 @@ def tile_rows_glin_kernel(tc, x, w_words, w_scales, out):
                     stop=True,
                 )
 
-        def empty(u, on_vector):
-            s, c0 = divmod(u * W, N)
+        def empty(u, on_vector, groups_a_store):
+            s, c0 = divmod(START[u], N)
+            w = WIDTH[u]
             for c in range(SIDE):
                 copy = nc.vector.tensor_copy if c in on_vector else nc.scalar.copy
-                copy(out=res[u][:, c, :], in_=banks[c][u % 2][:, N - W : N])
-                if c % 2 == 1:
-                    dst = out[SIDE * s + c - 1 : SIDE * s + c + 1, :, c0 : c0 + W].rearrange("c m n -> m c n")
-                    nc.sync.dma_start(out=dst, in_=res[u][:, c - 1 : c + 1, :])
+                copy(out=res[u][:, c, :], in_=banks[c][u % 2][:, N - w : N])
+                if (c + 1) % groups_a_store == 0:
+                    ca = c + 1 - groups_a_store
+                    dst = out[SIDE * s + ca : SIDE * s + c + 1, :, c0 : c0 + w].rearrange("c m n -> m c n")
+                    nc.sync.dma_start(out=dst, in_=res[u][:, ca : c + 1, :])
 
         for u in range(PIECES):
-            interleave(u)
+            interleave(u, 0 if u == PIECES - 1 else WIDTH[u] // 4)
             quantize(u)
             multiply(u)
             if u > 0:
-                empty(u - 1, (1,))
-        empty(PIECES - 1, (1, 3))
+                empty(u - 1, ((3,), (1,), (1, 3))[u - 1], 2 if u < 3 else 4)
+        empty(PIECES - 1, (1, 3), 4)

@@ -37,7 +37,7 @@ def tile_rows_glin_kernel(tc, x, w_words, w_scales, out):
         xsc = sb.tile([P, PAD + SETS * N], U8, name="xsc", align_bytes=64)
         raw = [sb.tile([P, PACK, w], F32, name="raw%d" % u, align_bytes=64) for u, w in enumerate(WIDTH)]
         grp = [sb.tile([P, w, PACK], BF16, name="grp%d" % u, align_bytes=64) for u, w in enumerate(WIDTH)]
-        res = [sb.tile([P, SIDE, w], F32, name="res%d" % u, align_bytes=64) for u, w in enumerate(WIDTH)]
+        res = [sb.tile([P, SIDE, N], F32, name="res%d" % s, align_bytes=64) for s in range(SETS)]
         banks = [[ps.tile([P, N], F32, name="bank%d_%d" % (c, h)) for h in range(2)] for c in range(SIDE)]
 
         nc.vector.memset(codes[:, 0:PAD], 0)
@@ -99,21 +99,35 @@ def tile_rows_glin_kernel(tc, x, w_words, w_scales, out):
                     stop=True,
                 )
 
-        def empty(u, on_vector, groups_a_store):
+        def empty(u, on_vector, on_scalar):
             s, c0 = divmod(START[u], N)
             w = WIDTH[u]
-            for c in range(SIDE):
-                copy = nc.vector.tensor_copy if c in on_vector else nc.scalar.copy
-                copy(out=res[u][:, c, :], in_=banks[c][u % 2][:, N - w : N])
-                if (c + 1) % groups_a_store == 0:
-                    ca = c + 1 - groups_a_store
-                    dst = out[SIDE * s + ca : SIDE * s + c + 1, :, c0 : c0 + w].rearrange("c m n -> m c n")
-                    nc.sync.dma_start(out=dst, in_=res[u][:, ca : c + 1, :])
+            for groups, copy in ((on_vector, nc.vector.tensor_copy), (on_scalar, nc.scalar.copy)):
+                for c in groups:
+                    copy(out=res[s][:, c, c0 : c0 + w], in_=banks[c][u % 2][:, N - w : N])
 
-        for u in range(PIECES):
+        def store(s, ca, cb, c0, c1):
+            dst = out[SIDE * s + ca : SIDE * s + cb, :, c0:c1].rearrange("c m n -> m c n")
+            nc.sync.dma_start(out=dst, in_=res[s][:, ca:cb, c0:c1])
+
+        def prepare(u):
             interleave(u, 0 if u == PIECES - 1 else WIDTH[u] // 4)
             quantize(u)
             multiply(u)
-            if u > 0:
-                empty(u - 1, ((3,), (1,), (1, 3))[u - 1], 2 if u < 3 else 4)
-        empty(PIECES - 1, (1, 3), 4)
+
+        half = N // 2
+        prepare(0)
+        prepare(1)
+        empty(0, (3,), (0, 1, 2))
+        store(0, 0, 2, 0, half)
+        store(0, 2, 4, 0, half)
+        prepare(2)
+        empty(1, (1,), (0, 2, 3))
+        store(0, 0, 2, half, N)
+        store(0, 2, 4, half, N)
+        prepare(3)
+        empty(2, (1, 3), (0, 2))
+        store(1, 0, 3, 0, half)
+        empty(3, (3, 2), (0, 1))
+        store(1, 3, 4, 0, N)
+        store(1, 0, 3, half, N)

@@ -84,10 +84,10 @@ def tile_rows_glin_kernel(tc, x, w_words, w_scales, out):
                 )
                 a = a + w
 
-        def multiply(u):
+        def multiply(u, order):
             s = START[u] // N
             end = PAD + START[u] + WIDTH[u]
-            for c in range(SIDE):
+            for c in order:
                 rows = slice(ROWS * c, ROWS * (c + 1))
                 nc.tensor.matmul_mx(
                     out=banks[c][u % 2][:],
@@ -113,7 +113,7 @@ def tile_rows_glin_kernel(tc, x, w_words, w_scales, out):
         def prepare(u):
             interleave(u, 0 if u == PIECES - 1 else WIDTH[u] // 4)
             quantize(u)
-            multiply(u)
+            multiply(u, (3, 0, 1, 2) if u == PIECES - 1 else range(SIDE))
 
         half = N // 2
         prepare(0)
@@ -126,8 +126,8 @@ def tile_rows_glin_kernel(tc, x, w_words, w_scales, out):
         store(0, 0, 2, half, N)
         store(0, 2, 4, half, N)
         prepare(3)
-        empty(2, (1, 3), (0, 2))
+        empty(2, (1,), (0, 2, 3))
         store(1, 0, 3, 0, half)
-        empty(3, (3, 2), (0, 1))
+        empty(3, (0, 2), (3, 1))
         store(1, 3, 4, 0, N)
         store(1, 0, 3, half, N)

@@ -55,10 +55,10 @@ def tile_rows_glin_kernel(tc, x, w_words, w_scales, out):
             out=words[:].bitcast(I32),
             in_=w_words.rearrange("g p b -> (g p) b").rearrange("(s q) b -> q s b", s=SETS).bitcast(I32),
         )
-        for f in range(4):
+        for c in range(SIDE):
             nc.sync.dma_start(
-                out=wsc[:].bitcast(I32)[f:P:ROWS],
-                in_=w_scales.rearrange("(s c) f m -> f c s m", s=SETS)[f].bitcast(I32),
+                out=wsc[:].bitcast(I32)[ROWS * c : ROWS * c + 4],
+                in_=w_scales.rearrange("(s c) f m -> c f s m", s=SETS)[c].bitcast(I32),
             )
         for u in range(1, PIECES):
             load(u)

@@ -31,13 +31,13 @@ def tile_rows_glin_kernel(tc, x, w_words, w_scales, out):
         ps = ctx.enter_context(tc.psum_pool(name="ps", bufs=1))
         ctx.enter_context(tc.manual_schedule())
 
-        words = sb.tile([P, SETS, 2 * M], U8, name="words", align_bytes=64)
-        wsc = sb.tile([P, SETS, M], U8, name="wsc", align_bytes=64)
-        codes = sb.tile([P, PAD + SETS * N], I32, name="codes", align_bytes=64)
-        xsc = sb.tile([P, PAD + SETS * N], U8, name="xsc", align_bytes=64)
-        raw = [sb.tile([P, PACK, w], F32, name="raw%d" % u, align_bytes=64) for u, w in enumerate(WIDTH)]
-        grp = [sb.tile([P, w, PACK], BF16, name="grp%d" % u, align_bytes=64) for u, w in enumerate(WIDTH)]
-        res = [sb.tile([P, SIDE, N], F32, name="res%d" % s, align_bytes=64) for s in range(SETS)]
+        words = sb.tile([P, SETS, 2 * M], U8, name="words", align_bytes=256)
+        wsc = sb.tile([P, SETS, M], U8, name="wsc", align_bytes=256)
+        codes = sb.tile([P, PAD + SETS * N], I32, name="codes", align_bytes=256)
+        xsc = sb.tile([P, PAD + SETS * N], U8, name="xsc", align_bytes=256)
+        raw = [sb.tile([P, PACK, w], F32, name="raw%d" % u, align_bytes=256) for u, w in enumerate(WIDTH)]
+        grp = [sb.tile([P, w, PACK], BF16, name="grp%d" % u, align_bytes=256) for u, w in enumerate(WIDTH)]
+        res = [sb.tile([P, SIDE, N], F32, name="res%d" % s, align_bytes=256) for s in range(SETS)]
         banks = [[ps.tile([P, N], F32, name="bank%d_%d" % (c, h)) for h in range(2)] for c in range(SIDE)]
 
         nc.vector.memset(codes[:, 0:PAD], 0)

@@ -17,7 +17,7 @@ PACK = 4
 ROWS = 32
 SIDE = 4
 SETS = 2
-CALLS = [(128, 128)] * 4
+CALLS = [(128, 128)] * 3 + [(128, 64, 64)]
 WIDTH = [sum(calls) for calls in CALLS]
 START = [sum(WIDTH[:u]) for u in range(len(WIDTH))]
 PIECES = len(WIDTH)
@@ -32,12 +32,12 @@ def tile_rows_glin_kernel(tc, x, w_words, w_scales, out):
         ctx.enter_context(tc.manual_schedule())
 
         words = sb.tile([P, SETS, 2 * M], U8, name="words", align_bytes=256)
-        wsc = sb.tile([P, SETS, M], U8, name="wsc", align_bytes=256)
+        wsc = sb.tile([P, SETS, 2 * M], U8, name="wsc", align_bytes=256)
         codes = sb.tile([P, PAD + SETS * N], I32, name="codes", align_bytes=256)
         xsc = sb.tile([P, PAD + SETS * N], U8, name="xsc", align_bytes=256)
-        raw = [sb.tile([P, PACK, w], F32, name="raw%d" % u, align_bytes=256) for u, w in enumerate(WIDTH)]
+        raw = [sb.tile([P, PACK, w], F32, name="raw%d" % u, align_bytes=1024) for u, w in enumerate(WIDTH)]
         grp = [sb.tile([P, w, PACK], BF16, name="grp%d" % u, align_bytes=256) for u, w in enumerate(WIDTH)]
-        res = [sb.tile([P, SIDE, N], F32, name="res%d" % s, align_bytes=256) for s in range(SETS)]
+        res = [sb.tile([P, SIDE, N], F32, name="res%d" % s, align_bytes=1024) for s in range(SETS)]
         banks = [[ps.tile([P, N], F32, name="bank%d_%d" % (c, h)) for h in range(2)] for c in range(SIDE)]
 
         nc.vector.memset(codes[:, 0:PAD], 0)
@@ -57,15 +57,16 @@ def tile_rows_glin_kernel(tc, x, w_words, w_scales, out):
         )
         for c in range(SIDE):
             nc.sync.dma_start(
-                out=wsc[:].bitcast(I32)[ROWS * c : ROWS * c + 4],
+                out=wsc[ROWS * c : ROWS * c + 4, :, 0:M].bitcast(I32),
                 in_=w_scales.rearrange("(s c) f m -> c f s m", s=SETS)[c].bitcast(I32),
             )
         for u in range(1, PIECES):
             load(u)
 
         def interleave(u, scalar_share):
-            first, split = CALLS[u][0], WIDTH[u] - scalar_share
-            shares = [(0, first, nc.vector.tensor_copy), (first, split, nc.vector.tensor_copy), (split, WIDTH[u], nc.scalar.copy)]
+            split = WIDTH[u] - scalar_share
+            ends = [min(split, sum(CALLS[u][: k + 1])) for k in range(len(CALLS[u]))]
+            shares = [(a, b, nc.vector.tensor_copy) for a, b in zip([0] + ends, ends)] + [(split, WIDTH[u], nc.scalar.copy)]
             for a, b, copy in shares:
                 if b > a:
                     copy(
@@ -92,7 +93,7 @@ def tile_rows_glin_kernel(tc, x, w_words, w_scales, out):
                 nc.tensor.matmul_mx(
                     out=banks[c][u % 2][:],
                     lhsT=words[rows, s, :].bitcast(FP4X4),
-                    lhsT_scale=wsc[rows, s, :],
+                    lhsT_scale=wsc[rows, s, 0:M],
                     rhs=codes[rows, end - N : end].bitcast(FP8X4),
                     rhs_scale=xsc[rows, end - N : end],
                     start=True,

@@ -116,19 +116,21 @@ def tile_rows_glin_kernel(tc, x, w_words, w_scales, out):
             quantize(u)
             multiply(u, (3, 0, 1, 2) if u == PIECES - 1 else range(SIDE))
 
-        half = N // 2
+        def store_halves(u, groups):
+            s, c0 = divmod(START[u], N)
+            for c in groups:
+                store(s, c, c + 1, c0, c0 + WIDTH[u])
+
         prepare(0)
         prepare(1)
         empty(0, (3,), (0, 1, 2))
-        store(0, 0, 2, 0, half)
-        store(0, 2, 4, 0, half)
+        store_halves(0, range(SIDE))
         prepare(2)
-        empty(1, (1,), (0, 2, 3))
-        store(0, 0, 2, half, N)
-        store(0, 2, 4, half, N)
+        empty(1, (3,), (0, 1, 2))
+        store_halves(1, range(SIDE))
         prepare(3)
-        empty(2, (1,), (0, 2, 3))
-        store(1, 0, 3, 0, half)
+        empty(2, (2,), (0, 1, 3))
+        store_halves(2, range(SIDE - 1))
         empty(3, (0, 2), (3, 1))
         store(1, 3, 4, 0, N)
-        store(1, 0, 3, half, N)
+        store_halves(3, range(SIDE - 1))

@@ -114,7 +114,7 @@ def tile_rows_glin_kernel(tc, x, w_words, w_scales, out):
         def prepare(u):
             interleave(u, 0 if u == PIECES - 1 else WIDTH[u] // 4)
             quantize(u)
-            multiply(u, (3, 0, 1, 2) if u == PIECES - 1 else range(SIDE))
+            multiply(u, range(SIDE))
 
         def store_halves(u, groups):
             s, c0 = divmod(START[u], N)
@@ -124,13 +124,13 @@ def tile_rows_glin_kernel(tc, x, w_words, w_scales, out):
         prepare(0)
         prepare(1)
         empty(0, (3,), (0, 1, 2))
-        store_halves(0, range(SIDE))
+        store_halves(0, (0, 1))
+        store(0, 2, 4, 0, WIDTH[0])
         prepare(2)
         empty(1, (3,), (0, 1, 2))
         store_halves(1, range(SIDE))
         prepare(3)
-        empty(2, (2,), (0, 1, 3))
-        store_halves(2, range(SIDE - 1))
-        empty(3, (0, 2), (3, 1))
-        store(1, 3, 4, 0, N)
-        store_halves(3, range(SIDE - 1))
+        empty(2, (3,), (0, 1, 2))
+        store_halves(2, range(SIDE))
+        empty(3, (1, 3), (0, 2))
+        store_halves(3, range(SIDE))

@@ -17,7 +17,7 @@ PACK = 4
 ROWS = 32
 SIDE = 4
 SETS = 2
-CALLS = [(128, 128)] * 3 + [(128, 64, 64)]
+CALLS = [(128, 64, 64)] * 4
 WIDTH = [sum(calls) for calls in CALLS]
 START = [sum(WIDTH[:u]) for u in range(len(WIDTH))]
 PIECES = len(WIDTH)
@@ -127,7 +127,7 @@ def tile_rows_glin_kernel(tc, x, w_words, w_scales, out):
         store_halves(0, (0, 1))
         store(0, 2, 4, 0, WIDTH[0])
         prepare(2)
-        empty(1, (3,), (0, 1, 2))
+        empty(1, (), (0, 1, 2, 3))
         store_halves(1, range(SIDE))
         prepare(3)
         empty(2, (3,), (0, 1, 2))

@@ -55,12 +55,18 @@ def tile_rows_glin_kernel(tc, x, w_words, w_scales, out):
             out=words[:].bitcast(I32),
             in_=w_words.rearrange("g p b -> (g p) b").rearrange("(s q) b -> q s b", s=SETS).bitcast(I32),
         )
-        for c in range(SIDE):
-            nc.sync.dma_start(
-                out=wsc[ROWS * c : ROWS * c + 4, :, 0:M].bitcast(I32),
-                in_=w_scales.rearrange("(s c) f m -> c f s m", s=SETS)[c].bitcast(I32),
-            )
-        for u in range(1, PIECES):
+
+        def load_scales(tiles):
+            for c in tiles:
+                nc.sync.dma_start(
+                    out=wsc[ROWS * c : ROWS * c + 4, :, 0:M].bitcast(I32),
+                    in_=w_scales.rearrange("(s c) f m -> c f s m", s=SETS)[c].bitcast(I32),
+                )
+
+        load_scales((0, 1))
+        load(1)
+        load_scales((2, 3))
+        for u in range(2, PIECES):
             load(u)
 
         def interleave(u, scalar_share):

@@ -17,7 +17,7 @@ PACK = 4
 ROWS = 32
 SIDE = 4
 SETS = 2
-CALLS = [(128, 64, 64)] * 4
+CALLS = [(128, 64, 64), (128, 64, 64), (64, 64), (128, 64), (128, 64)]
 WIDTH = [sum(calls) for calls in CALLS]
 START = [sum(WIDTH[:u]) for u in range(len(WIDTH))]
 PIECES = len(WIDTH)
@@ -118,25 +118,22 @@ def tile_rows_glin_kernel(tc, x, w_words, w_scales, out):
             nc.sync.dma_start(out=dst, in_=res[s][:, ca:cb, c0:c1])
 
         def prepare(u):
-            interleave(u, 0 if u == PIECES - 1 else WIDTH[u] // 4)
+            interleave(u, WIDTH[u] // 4 if u < 2 else 0)
             quantize(u)
             multiply(u, range(SIDE))
 
-        def store_halves(u, groups):
+        def finish(u):
             s, c0 = divmod(START[u], N)
-            for c in groups:
-                store(s, c, c + 1, c0, c0 + WIDTH[u])
+            if u < PIECES - 2:
+                empty(u, (), range(SIDE))
+            else:
+                empty(u, (1, 3), (0, 2))
+            step = 1 if s == 0 else 2
+            for c in range(0, SIDE, step):
+                store(s, c, c + step, c0, c0 + WIDTH[u])
 
         prepare(0)
-        prepare(1)
-        empty(0, (3,), (0, 1, 2))
-        store_halves(0, (0, 1))
-        store(0, 2, 4, 0, WIDTH[0])
-        prepare(2)
-        empty(1, (), (0, 1, 2, 3))
-        store_halves(1, range(SIDE))
-        prepare(3)
-        empty(2, (3,), (0, 1, 2))
-        store_halves(2, range(SIDE))
-        empty(3, (1, 3), (0, 2))
-        store_halves(3, range(SIDE))
+        for u in range(1, PIECES):
+            prepare(u)
+            finish(u - 1)
+        finish(PIECES - 1)

@@ -17,7 +17,7 @@ PACK = 4
 ROWS = 32
 SIDE = 4
 SETS = 2
-CALLS = [(128, 64, 64), (128, 64, 64), (64, 64), (128, 64), (128, 64)]
+CALLS = [(128, 64), (128, 64), (64, 64)] * SETS
 WIDTH = [sum(calls) for calls in CALLS]
 START = [sum(WIDTH[:u]) for u in range(len(WIDTH))]
 PIECES = len(WIDTH)
@@ -118,19 +118,16 @@ def tile_rows_glin_kernel(tc, x, w_words, w_scales, out):
             nc.sync.dma_start(out=dst, in_=res[s][:, ca:cb, c0:c1])
 
         def prepare(u):
-            interleave(u, WIDTH[u] // 4 if u < 2 else 0)
+            interleave(u, 64 if u < 2 else 0)
             quantize(u)
             multiply(u, range(SIDE))
 
         def finish(u):
             s, c0 = divmod(START[u], N)
-            if u < PIECES - 2:
-                empty(u, (), range(SIDE))
-            else:
-                empty(u, (1, 3), (0, 2))
-            step = 1 if s == 0 else 2
-            for c in range(0, SIDE, step):
-                store(s, c, c + step, c0, c0 + WIDTH[u])
+            on_vector = ((), (), (), (1,), (1, 3), (1, 3))[u]
+            empty(u, on_vector, [c for c in range(SIDE) if c not in on_vector])
+            for ca, cb in ((0, 1), (1, 2), (2, 4)) if u == 0 else ((0, 2), (2, 4)):
+                store(s, ca, cb, c0, c0 + WIDTH[u])
 
         prepare(0)
         for u in range(1, PIECES):

@@ -17,7 +17,7 @@ PACK = 4
 ROWS = 32
 SIDE = 4
 SETS = 2
-CALLS = [(128, 64), (128, 64), (64, 64)] * SETS
+CALLS = [(64, 64, 64), (64, 64, 64), (64, 64), (128, 64), (128, 64), (64, 64)]
 WIDTH = [sum(calls) for calls in CALLS]
 START = [sum(WIDTH[:u]) for u in range(len(WIDTH))]
 PIECES = len(WIDTH)
@@ -117,17 +117,22 @@ def tile_rows_glin_kernel(tc, x, w_words, w_scales, out):
             dst = out[SIDE * s + ca : SIDE * s + cb, :, c0:c1].rearrange("c m n -> m c n")
             nc.sync.dma_start(out=dst, in_=res[s][:, ca:cb, c0:c1])
 
+        def tiles(u):
+            return list(range(SIDE)) if u % 2 == 0 else list(range(SIDE - 1, -1, -1))
+
         def prepare(u):
             interleave(u, 64 if u < 2 else 0)
             quantize(u)
-            multiply(u, range(SIDE))
+            multiply(u, tiles(u))
 
         def finish(u):
             s, c0 = divmod(START[u], N)
-            on_vector = ((), (), (), (1,), (1, 3), (1, 3))[u]
-            empty(u, on_vector, [c for c in range(SIDE) if c not in on_vector])
-            for ca, cb in ((0, 1), (1, 2), (2, 4)) if u == 0 else ((0, 2), (2, 4)):
-                store(s, ca, cb, c0, c0 + WIDTH[u])
+            order = tiles(u)
+            on_vector = [order[i] for i in ((), (), (), (1,), (1, 3), (1, 3))[u]]
+            empty(u, on_vector, [c for c in order if c not in on_vector])
+            runs = [order[0:1], order[1:2], order[2:4]] if u == 1 else [order[0:2], order[2:4]]
+            for run in runs:
+                store(s, min(run), max(run) + 1, c0, c0 + WIDTH[u])
 
         prepare(0)
         for u in range(1, PIECES):

@@ -17,11 +17,11 @@ PACK = 4
 ROWS = 32
 SIDE = 4
 SETS = 2
-CALLS = [(64, 64, 64), (64, 64, 64), (64, 64), (128, 64), (128, 64), (64, 64)]
-WIDTH = [sum(calls) for calls in CALLS]
-START = [sum(WIDTH[:u]) for u in range(len(WIDTH))]
-PIECES = len(WIDTH)
-PAD = N - WIDTH[0]
+WIDTH = 128
+PIECES = SETS * N // WIDTH
+HALF = WIDTH // 2
+PAD = N - WIDTH
+RUNS = {0: [(0, 2), (2, 4)], 1: [(0, 2), (2, 4)], 2: [(0, 2), (2, 4)]}
 
 
 def tile_rows_glin_kernel(tc, x, w_words, w_scales, out):
@@ -35,9 +35,9 @@ def tile_rows_glin_kernel(tc, x, w_words, w_scales, out):
         wsc = sb.tile([P, SETS, 2 * M], U8, name="wsc", align_bytes=256)
         codes = sb.tile([P, PAD + SETS * N], I32, name="codes", align_bytes=256)
         xsc = sb.tile([P, PAD + SETS * N], U8, name="xsc", align_bytes=256)
-        raw = [sb.tile([P, PACK, w], F32, name="raw%d" % u, align_bytes=1024) for u, w in enumerate(WIDTH)]
-        grp = [sb.tile([P, w, PACK], BF16, name="grp%d" % u, align_bytes=256) for u, w in enumerate(WIDTH)]
-        res = [sb.tile([P, SIDE, N], F32, name="res%d" % s, align_bytes=1024) for s in range(SETS)]
+        raw = [sb.tile([P, PACK, WIDTH], F32, name="raw%d" % u, align_bytes=1024) for u in range(PIECES)]
+        grp = [sb.tile([P, WIDTH, PACK], BF16, name="grp%d" % u, align_bytes=256) for u in range(PIECES)]
+        res = [sb.tile([P, SIDE, WIDTH], F32, name="res%d" % u, align_bytes=1024) for u in range(PIECES)]
         banks = [[ps.tile([P, N], F32, name="bank%d_%d" % (c, h)) for h in range(2)] for c in range(SIDE)]
 
         nc.vector.memset(codes[:, 0:PAD], 0)
@@ -46,15 +46,9 @@ def tile_rows_glin_kernel(tc, x, w_words, w_scales, out):
         x_rows = x.rearrange("g d n -> (g d) n")
 
         def load(u):
-            s, c0 = divmod(START[u], N)
+            s, c0 = divmod(u * WIDTH, N)
             src = x_rows[s * P * PACK : (s + 1) * P * PACK, :].rearrange("(q j) n -> q j n", j=PACK)
-            nc.sync.dma_start(out=raw[u][:], in_=src[:, :, c0 : c0 + WIDTH[u]])
-
-        load(0)
-        nc.sync.dma_start(
-            out=words[:].bitcast(I32),
-            in_=w_words.rearrange("g p b -> (g p) b").rearrange("(s q) b -> q s b", s=SETS).bitcast(I32),
-        )
+            nc.sync.dma_start(out=raw[u][:], in_=src[:, :, c0 : c0 + WIDTH])
 
         def load_scales(tiles):
             for c in tiles:
@@ -63,38 +57,34 @@ def tile_rows_glin_kernel(tc, x, w_words, w_scales, out):
                     in_=w_scales.rearrange("(s c) f m -> c f s m", s=SETS)[c].bitcast(I32),
                 )
 
+        load(0)
+        nc.sync.dma_start(
+            out=words[:].bitcast(I32),
+            in_=w_words.rearrange("g p b -> (g p) b").rearrange("(s q) b -> q s b", s=SETS).bitcast(I32),
+        )
         load_scales((0, 1))
         load(1)
         load_scales((2, 3))
         for u in range(2, PIECES):
             load(u)
 
-        def interleave(u, scalar_share):
-            split = WIDTH[u] - scalar_share
-            ends = [min(split, sum(CALLS[u][: k + 1])) for k in range(len(CALLS[u]))]
-            shares = [(a, b, nc.vector.tensor_copy) for a, b in zip([0] + ends, ends)] + [(split, WIDTH[u], nc.scalar.copy)]
-            for a, b, copy in shares:
-                if b > a:
-                    copy(
-                        out=grp[u][:, a:b, :].rearrange("p (c i) t -> p c t i", i=4),
-                        in_=raw[u][:, :, a:b].rearrange("p t (c i) -> p c t i", i=4),
-                    )
-
-        def quantize(u):
-            a = 0
-            for w in CALLS[u]:
-                at = PAD + START[u] + a
-                nc.vector.quantize_mx(
-                    out=codes[:, at : at + w].bitcast(FP8X4),
-                    scales=xsc[:, at : at + w],
-                    in_=grp[u][:, a : a + w, :].rearrange("p n t -> p (n t)"),
+        def prepare(u):
+            second = nc.scalar.copy if u < 2 else nc.vector.tensor_copy
+            for a, copy in ((0, nc.vector.tensor_copy), (HALF, second)):
+                copy(
+                    out=grp[u][:, a : a + HALF, :].rearrange("p (c i) t -> p c t i", i=4),
+                    in_=raw[u][:, :, a : a + HALF].rearrange("p t (c i) -> p c t i", i=4),
                 )
-                a = a + w
-
-        def multiply(u, order):
-            s = START[u] // N
-            end = PAD + START[u] + WIDTH[u]
-            for c in order:
+            for a in (0, HALF):
+                at = PAD + u * WIDTH + a
+                nc.vector.quantize_mx(
+                    out=codes[:, at : at + HALF].bitcast(FP8X4),
+                    scales=xsc[:, at : at + HALF],
+                    in_=grp[u][:, a : a + HALF, :].rearrange("p n t -> p (n t)"),
+                )
+            s = u * WIDTH // N
+            end = PAD + (u + 1) * WIDTH
+            for c in range(SIDE):
                 rows = slice(ROWS * c, ROWS * (c + 1))
                 nc.tensor.matmul_mx(
                     out=banks[c][u % 2][:],
@@ -106,33 +96,14 @@ def tile_rows_glin_kernel(tc, x, w_words, w_scales, out):
                     stop=True,
                 )
 
-        def empty(u, on_vector, on_scalar):
-            s, c0 = divmod(START[u], N)
-            w = WIDTH[u]
-            for groups, copy in ((on_vector, nc.vector.tensor_copy), (on_scalar, nc.scalar.copy)):
-                for c in groups:
-                    copy(out=res[s][:, c, c0 : c0 + w], in_=banks[c][u % 2][:, N - w : N])
-
-        def store(s, ca, cb, c0, c1):
-            dst = out[SIDE * s + ca : SIDE * s + cb, :, c0:c1].rearrange("c m n -> m c n")
-            nc.sync.dma_start(out=dst, in_=res[s][:, ca:cb, c0:c1])
-
-        def tiles(u):
-            return list(range(SIDE)) if u % 2 == 0 else list(range(SIDE - 1, -1, -1))
-
-        def prepare(u):
-            interleave(u, 64 if u < 2 else 0)
-            quantize(u)
-            multiply(u, tiles(u))
-
         def finish(u):
-            s, c0 = divmod(START[u], N)
-            order = tiles(u)
-            on_vector = [order[i] for i in ((), (), (), (1,), (1, 3), (1, 3))[u]]
-            empty(u, on_vector, [c for c in order if c not in on_vector])
-            runs = [order[0:1], order[1:2], order[2:4]] if u == 1 else [order[0:2], order[2:4]]
-            for run in runs:
-                store(s, min(run), max(run) + 1, c0, c0 + WIDTH[u])
+            s, c0 = divmod(u * WIDTH, N)
+            for c in range(SIDE):
+                copy = nc.vector.tensor_copy if u >= PIECES - 2 and c % 2 else nc.scalar.copy
+                copy(out=res[u][:, c, :], in_=banks[c][u % 2][:, N - WIDTH : N])
+            for ca, cb in RUNS.get(u, [(0, SIDE)]):
+                dst = out[SIDE * s + ca : SIDE * s + cb, :, c0 : c0 + WIDTH].rearrange("c m n -> m c n")
+                nc.sync.dma_start(out=dst, in_=res[u][:, ca:cb, :])
 
         prepare(0)
         for u in range(1, PIECES):

@@ -21,7 +21,6 @@ WIDTH = 128
 PIECES = SETS * N // WIDTH
 HALF = WIDTH // 2
 PAD = N - WIDTH
-RUNS = {0: [(0, 2), (2, 4)], 1: [(0, 2), (2, 4)], 2: [(0, 2), (2, 4)]}
 
 
 def tile_rows_glin_kernel(tc, x, w_words, w_scales, out):
@@ -37,7 +36,7 @@ def tile_rows_glin_kernel(tc, x, w_words, w_scales, out):
         xsc = sb.tile([P, PAD + SETS * N], U8, name="xsc", align_bytes=256)
         raw = [sb.tile([P, PACK, WIDTH], F32, name="raw%d" % u, align_bytes=1024) for u in range(PIECES)]
         grp = [sb.tile([P, WIDTH, PACK], BF16, name="grp%d" % u, align_bytes=256) for u in range(PIECES)]
-        res = [sb.tile([P, SIDE, WIDTH], F32, name="res%d" % u, align_bytes=1024) for u in range(PIECES)]
+        res = [sb.tile([P, SIDE, N], F32, name="res%d" % s, align_bytes=1024) for s in range(SETS)]
         banks = [[ps.tile([P, N], F32, name="bank%d_%d" % (c, h)) for h in range(2)] for c in range(SIDE)]
 
         nc.vector.memset(codes[:, 0:PAD], 0)
@@ -68,6 +67,9 @@ def tile_rows_glin_kernel(tc, x, w_words, w_scales, out):
         for u in range(2, PIECES):
             load(u)
 
+        def tiles(u):
+            return (0, 1, 2, 3) if u % 2 == 0 else (2, 3, 0, 1)
+
         def prepare(u):
             second = nc.scalar.copy if u < 2 else nc.vector.tensor_copy
             for a, copy in ((0, nc.vector.tensor_copy), (HALF, second)):
@@ -84,7 +86,7 @@ def tile_rows_glin_kernel(tc, x, w_words, w_scales, out):
                 )
             s = u * WIDTH // N
             end = PAD + (u + 1) * WIDTH
-            for c in range(SIDE):
+            for c in tiles(u):
                 rows = slice(ROWS * c, ROWS * (c + 1))
                 nc.tensor.matmul_mx(
                     out=banks[c][u % 2][:],
@@ -96,14 +98,23 @@ def tile_rows_glin_kernel(tc, x, w_words, w_scales, out):
                     stop=True,
                 )
 
+        def store(s, ca, cb, c0, c1):
+            dst = out[SIDE * s + ca : SIDE * s + cb, :, c0:c1].rearrange("c m n -> m c n")
+            nc.sync.dma_start(out=dst, in_=res[s][:, ca:cb, c0:c1])
+
         def finish(u):
             s, c0 = divmod(u * WIDTH, N)
-            for c in range(SIDE):
+            c1 = c0 + WIDTH
+            for c in tiles(u):
                 copy = nc.vector.tensor_copy if u >= PIECES - 2 and c % 2 else nc.scalar.copy
-                copy(out=res[u][:, c, :], in_=banks[c][u % 2][:, N - WIDTH : N])
-            for ca, cb in RUNS.get(u, [(0, SIDE)]):
-                dst = out[SIDE * s + ca : SIDE * s + cb, :, c0 : c0 + WIDTH].rearrange("c m n -> m c n")
-                nc.sync.dma_start(out=dst, in_=res[u][:, ca:cb, :])
+                copy(out=res[s][:, c, c0:c1], in_=banks[c][u % 2][:, N - WIDTH : N])
+            first, second = tiles(u)[0], tiles(u)[2]
+            if u == PIECES - 1:
+                store(s, 0, SIDE, c0, c1)
+                return
+            store(s, first, first + 2, max(0, c0 - WIDTH), c1)
+            if c1 == N or u == PIECES - 2:
+                store(s, second, second + 2, c0, c1)
 
         prepare(0)
         for u in range(1, PIECES):

@@ -109,10 +109,7 @@ def tile_rows_glin_kernel(tc, x, w_words, w_scales, out):
                 copy = nc.vector.tensor_copy if u >= PIECES - 2 and c % 2 else nc.scalar.copy
                 copy(out=res[s][:, c, c0:c1], in_=banks[c][u % 2][:, N - WIDTH : N])
             first, second = tiles(u)[0], tiles(u)[2]
-            if u == PIECES - 1:
-                store(s, 0, SIDE, c0, c1)
-                return
-            store(s, first, first + 2, max(0, c0 - WIDTH), c1)
+            store(s, first, first + 2, c0 if u == PIECES - 1 else max(0, c0 - WIDTH), c1)
             if c1 == N or u == PIECES - 2:
                 store(s, second, second + 2, c0, c1)
 

from contextlib import ExitStack

import concourse.mybir as mybir

G, D, M, N = 8, 128, 128, 512
FLOPS = 2 * G * D * M * N

F32 = mybir.dt.float32
BF16 = mybir.dt.bfloat16
I32 = mybir.dt.int32
U8 = mybir.dt.uint8
FP8X4 = mybir.dt.float8_e4m3fn_x4
FP4X4 = mybir.dt.float4_e2m1fn_x4

P = 128
PACK = 4
ROWS = 32
SIDE = 4
SETS = 2
WIDTH = 128
PIECES = SETS * N // WIDTH
HALF = WIDTH // 2
PAD = N - WIDTH


def tile_rows_glin_kernel(tc, x, w_words, w_scales, out):
    nc = tc.nc
    with ExitStack() as ctx:
        sb = ctx.enter_context(tc.tile_pool(name="sb", bufs=1))
        ps = ctx.enter_context(tc.psum_pool(name="ps", bufs=1))
        ctx.enter_context(tc.manual_schedule())

        words = sb.tile([P, SETS, 2 * M], U8, name="words", align_bytes=256)
        wsc = sb.tile([P, SETS, 2 * M], U8, name="wsc", align_bytes=256)
        codes = sb.tile([P, PAD + SETS * N], I32, name="codes", align_bytes=256)
        xsc = sb.tile([P, PAD + SETS * N], U8, name="xsc", align_bytes=256)
        raw = [sb.tile([P, PACK, WIDTH], F32, name="raw%d" % u, align_bytes=1024) for u in range(PIECES)]
        grp = [sb.tile([P, WIDTH, PACK], BF16, name="grp%d" % u, align_bytes=256) for u in range(PIECES)]
        res = [sb.tile([P, SIDE, N], F32, name="res%d" % s, align_bytes=1024) for s in range(SETS)]
        banks = [[ps.tile([P, N], F32, name="bank%d_%d" % (c, h)) for h in range(2)] for c in range(SIDE)]

        nc.vector.memset(codes[:, 0:PAD], 0)
        nc.vector.memset(xsc[:, 0:PAD].bitcast(I32), 0)

        x_rows = x.rearrange("g d n -> (g d) n")

        def load(u):
            s, c0 = divmod(u * WIDTH, N)
            src = x_rows[s * P * PACK : (s + 1) * P * PACK, :].rearrange("(q j) n -> q j n", j=PACK)
            nc.sync.dma_start(out=raw[u][:], in_=src[:, :, c0 : c0 + WIDTH])

        def load_scales(tiles):
            for c in tiles:
                nc.sync.dma_start(
                    out=wsc[ROWS * c : ROWS * c + 4, :, 0:M].bitcast(I32),
                    in_=w_scales.rearrange("(s c) f m -> c f s m", s=SETS)[c].bitcast(I32),
                )

        load(0)
        nc.sync.dma_start(
            out=words[:].bitcast(I32),
            in_=w_words.rearrange("g p b -> (g p) b").rearrange("(s q) b -> q s b", s=SETS).bitcast(I32),
        )
        load_scales((0, 1))
        load(1)
        load_scales((2, 3))
        for u in range(2, PIECES):
            load(u)

        def tiles(u):
            return (0, 1, 2, 3) if u % 2 == 0 else (2, 3, 0, 1)

        def prepare(u):
            second = nc.scalar.copy if u < 2 else nc.vector.tensor_copy
            for a, copy in ((0, nc.vector.tensor_copy), (HALF, second)):
                copy(
                    out=grp[u][:, a : a + HALF, :].rearrange("p (c i) t -> p c t i", i=4),
                    in_=raw[u][:, :, a : a + HALF].rearrange("p t (c i) -> p c t i", i=4),
                )
            for a in (0, HALF):
                at = PAD + u * WIDTH + a
                nc.vector.quantize_mx(
                    out=codes[:, at : at + HALF].bitcast(FP8X4),
                    scales=xsc[:, at : at + HALF],
                    in_=grp[u][:, a : a + HALF, :].rearrange("p n t -> p (n t)"),
                )
            s = u * WIDTH // N
            end = PAD + (u + 1) * WIDTH
            for c in tiles(u):
                rows = slice(ROWS * c, ROWS * (c + 1))
                nc.tensor.matmul_mx(
                    out=banks[c][u % 2][:],
                    lhsT=words[rows, s, :].bitcast(FP4X4),
                    lhsT_scale=wsc[rows, s, 0:M],
                    rhs=codes[rows, end - N : end].bitcast(FP8X4),
                    rhs_scale=xsc[rows, end - N : end],
                    start=True,
                    stop=True,
                )

        def store(s, ca, cb, c0, c1):
            dst = out[SIDE * s + ca : SIDE * s + cb, :, c0:c1].rearrange("c m n -> m c n")
            nc.sync.dma_start(out=dst, in_=res[s][:, ca:cb, c0:c1])

        def finish(u):
            s, c0 = divmod(u * WIDTH, N)
            c1 = c0 + WIDTH
            for c in tiles(u):
                copy = nc.vector.tensor_copy if u >= PIECES - 2 and c % 2 else nc.scalar.copy
                copy(out=res[s][:, c, c0:c1], in_=banks[c][u % 2][:, N - WIDTH : N])
            first, second = tiles(u)[0], tiles(u)[2]
            store(s, first, first + 2, c0 if u == PIECES - 1 else max(0, c0 - WIDTH), c1)
            if c1 == N or u == PIECES - 2:
                store(s, second, second + 2, c0, c1)

        prepare(0)
        for u in range(1, PIECES):
            prepare(u)
            finish(u - 1)
        finish(PIECES - 1)
